import numpy as np
import ml_dtypes


def mxq(x, axis, fmt="e4m3"):
    dtype, down = {"e4m3": (ml_dtypes.float8_e4m3fn, 7), "e5m2": (ml_dtypes.float8_e5m2, 14)}[fmt]
    v = np.moveaxis(np.asarray(x, np.float32).astype(ml_dtypes.bfloat16).astype(np.float64), axis, -1)
    blocks = v.reshape(v.shape[:-1] + (-1, 32))
    amax = np.abs(blocks).max(-1, keepdims=True)
    byte = np.maximum(np.where(amax > 0, np.frexp(amax)[1] - 1 + 127, 0) - down, 1)
    scale = np.exp2(byte - 127.0)
    codes = (blocks / scale).astype(np.float32).astype(dtype).astype(np.float64)
    return np.moveaxis((codes * scale).reshape(v.shape), -1, axis)


WIDE = False


def mx_kscale(k):
    if not WIDE:
        return np.ones(k)
    levels = np.array([30, -30])
    if k % 512:
        return np.exp2(np.random.permutation(np.resize(levels, k // 32))).repeat(32)
    a = np.empty((k // 512, 16))
    for p in range(k // 512):
        a[p, :8] = np.random.permutation(np.resize(levels, 8))
        for g in range(8):
            far = levels[np.abs(levels - a[p, g]) >= 10]
            a[p, g + 8] = far[np.random.randint(len(far))]
    return np.exp2(a.ravel()).repeat(32)


def f64(x):
    return np.asarray(x).astype(np.float64)


def striped8(idx):
    return np.asarray(idx).reshape(8, -1, 16).transpose(0, 2, 1).reshape(128, -1).astype(np.uint16)


def unstriped8(offs):
    return offs.reshape(8, 16, -1).transpose(0, 2, 1).reshape(8, -1).astype(np.int64)


def pick8(x, idx, run):
    r = np.arange(len(x))
    return x[r[:, None], idx[r % (8 * run) // run]]


E2M1 = np.array([0.0, 0.5, 1.0, 1.5, 2.0, 3.0, 4.0, 6.0, -0.0, -0.5, -1.0, -1.5, -2.0, -3.0, -4.0, -6.0])


def pack_weight(w, fmt):
    k, n = w.shape
    w = f64(np.asarray(w, np.float32).astype(ml_dtypes.bfloat16)).reshape(k // 32, 32, n)
    amax = np.abs(w).max(1)
    if fmt in ("e4m3", "e5m2"):
        byte = np.frexp(amax)[1] - 1 + 127 - (7 if fmt == "e4m3" else 14)
    else:
        mant, ex = np.frexp(amax / 6.0)
        byte = np.where(mant > 0.5, ex, ex - 1) + 127
    byte = np.clip(np.where(amax > 0, byte, 1), 1, 254)
    scaled = (w * np.exp2(127.0 - byte)[:, None, :]).reshape(k, n).astype(np.float32)
    by_word = np.ascontiguousarray(scaled.reshape(k // 512, 128, 4, n).transpose(0, 1, 3, 2))
    if fmt in ("e4m3", "e5m2"):
        words = by_word.astype(ml_dtypes.float8_e4m3fn if fmt == "e4m3" else ml_dtypes.float8_e5m2).view(np.uint8)
    else:
        c = by_word.astype(ml_dtypes.float4_e2m1fn).view(np.uint8) & 0xF
        words = (c[..., 0::2] | (c[..., 1::2] << 4)).reshape(k // 512, 128, 2 * n)
    return np.ascontiguousarray(words), np.ascontiguousarray(byte.astype(np.uint8).reshape(k // 512, 16, n))


def unpack_weight(words, scales, fmt):
    g, _, n = scales.shape
    words = np.ascontiguousarray(words).reshape(g, 128, n, -1)
    if fmt in ("e4m3", "e5m2"):
        vals = words.view(ml_dtypes.float8_e4m3fn if fmt == "e4m3" else ml_dtypes.float8_e5m2).astype(np.float64)
    else:
        nib = np.empty((g, 128, n, 4), np.uint8)
        nib[..., 0::2] = words & 0xF
        nib[..., 1::2] = words >> 4
        vals = E2M1[nib]
    vals = vals * np.repeat(np.exp2(scales.astype(np.float64) - 127.0), 8, axis=1)[..., None]
    return vals.transpose(0, 1, 3, 2).reshape(g * 512, n)


K, T, J, R, F, N, Q = 512, 512, 256, 512, 512, 256, 64


def setup_inputs():
    n = np.random.standard_normal
    idx = np.stack([np.random.permutation(T)[:J] for _ in range(8)])
    fk = mx_kscale(K)
    fr = mx_kscale(R)
    ff = mx_kscale(F)
    xtp = pack_weight(n((K, T)) / fk[:, None], "e5m2")
    wp = pack_weight(n((K, R)) * 1 / np.sqrt(K) * fk[:, None] * fr, "e2m1")
    w2p = pack_weight(n((F, R)) * 1 / np.sqrt(F) * ff[:, None] * fr, "e2m1")
    wbp = pack_weight(n((R, N)) * 1 / np.sqrt(R) / fr[:, None], "e4m3")
    return {
        "xt_words": xtp[0],
        "xt_scales": xtp[1],
        "w_words": wp[0],
        "w_scales": wp[1],
        "so": (n((F, J))).astype(np.float32),
        "fl": (np.random.uniform(0.5, 2.0, (F, 1)) / ff[:, None]).astype(np.float32),
        "w2_words": w2p[0],
        "w2_scales": w2p[1],
        "wb_words": wbp[0],
        "wb_scales": wbp[1],
        "rw": (np.random.uniform(0.5, 2.0, (1, J))).astype(np.float32),
        "qw": (np.random.uniform(0.5, 2.0, (1, Q))).astype(np.float32),
        "offs": striped8(idx),
    }


def reference(xt_words, xt_scales, w_words, w_scales, so, fl, w2_words, w2_scales, wb_words, wb_scales, rw, qw, offs):
    idx = unstriped8(offs)
    xtu = unpack_weight(xt_words, xt_scales, "e5m2")
    wu = unpack_weight(w_words, w_scales, "e2m1")
    w2u = unpack_weight(w2_words, w2_scales, "e2m1")
    wbu = unpack_weight(wb_words, wb_scales, "e4m3")
    s1 = np.pad(f64(so), ((0, 0), (1, 0)))[:, :J]
    u2 = (f64(so) - 0.8 * s1) * f64(fl)
    xtidxg = pick8(xtu, idx, 64)
    u2q = mxq(u2, 0, "e4m3")
    a = wu.T @ xtidxg + w2u.T @ u2q
    hid = np.maximum(a, 0.0)
    hidq = mxq(hid, 0, "e5m2")
    p = wbu.T @ hidq
    y = (p * f64(rw)).reshape(N, Q, J // Q).sum(axis=2) * f64(qw)
    return y

@@ -1,0 +1,188 @@
+from contextlib import ExitStack
+
+import concourse.mybir as mybir
+from concourse.masks import make_identity
+
+K, T, J, R, F, N, Q = 512, 512, 256, 512, 512, 256, 64
+FLOPS = 2 * (K * R * J + F * R * J + R * N * J)
+
+F32 = mybir.dt.float32
+BF16 = mybir.dt.bfloat16
+I32 = mybir.dt.int32
+U32 = mybir.dt.uint32
+U16 = mybir.dt.uint16
+U8 = mybir.dt.uint8
+E4M3 = mybir.dt.float8_e4m3fn_x4
+E5M2 = mybir.dt.float8_e5m2_x4
+E2M1 = mybir.dt.float4_e2m1fn_x4
+ALU = mybir.AluOpType
+ACT = mybir.ActivationFunctionType
+
+P = 128
+HALF = 128
+PAD = 4
+W_COL, W2_COL, X_COL, WB_COL, PLANE = 0, 512, 1024, 1280, 1536
+
+
+def tile_list_sum_headpicks_stepped_plain_groupsums_kernel(
+    tc, xt_words, xt_scales, w_words, w_scales, so, fl, w2_words, w2_scales, wb_words, wb_scales, rw, qw, offs, out
+):
+    nc = tc.nc
+    with ExitStack() as ctx:
+        sb = ctx.enter_context(tc.tile_pool(name="sb", bufs=1))
+        ps = ctx.enter_context(tc.psum_pool(name="ps", bufs=1))
+
+        def tile(name, shape, dtype):
+            return sb.tile(shape, dtype, name=name, align_bytes=64)
+
+        offsets = sb.tile([P, J // 16], U16, name="offsets")
+        nc.sync.dma_start(offsets[:], offs)
+
+        x_scale_win = tile("x_scale_win", [P, T], U8)
+        w_scale_raw = [tile(f"w_scale_raw{s}", [P, R], U8) for s in range(2)]
+        staged = tile("staged", [P, PLANE], U8)
+        plane = tile("plane", [P, PLANE], U8)
+        zero = tile("zero", [P, 2, 1], F32)
+        nc.vector.memset(zero[:], 0.0)
+        nc.sync.dma_start(x_scale_win[:].bitcast(I32), xt_scales[0].bitcast(I32).unsqueeze(1).to_broadcast([16, 8, T // 4]))
+        fl_t = tile("fl_t", [P, 4], F32)
+        nc.sync.dma_start(fl_t[:], fl.rearrange("(p t) o -> p (t o)", t=4))
+        for s, scales in enumerate((w_scales, w2_scales)):
+            nc.scalar.dma_start(w_scale_raw[s][:].bitcast(I32), scales[0].bitcast(I32).unsqueeze(1).to_broadcast([16, 8, R // 4]))
+
+        so_rows = so.rearrange("(p t) j -> p t j", t=4)
+        so_t = [tile(f"so{e}", [P, 2, J], F32) for e in range(2)]
+        for e in range(2):
+            nc.sync.dma_start(so_t[e][:], so_rows[:, 2 * e : 2 * e + 2, :])
+        w_raw = [tile(f"w_raw{s}", [P, 2 * R], U8) for s in range(2)]
+        for s, words in ((1, w2_words), (0, w_words)):
+            nc.sync.dma_start(w_raw[s][:].bitcast(I32), words[0].bitcast(I32))
+        x_word_win = tile("x_word_win", [P, T], I32)
+        nc.sync.dma_start(x_word_win[:], xt_words[0].rearrange("p n t -> p (n t)").bitcast(I32))
+        wb_t = tile("wb_t", [P, N], I32)
+        nc.sync.dma_start(wb_t[:], wb_words[0].rearrange("p n t -> p (n t)").bitcast(I32))
+
+        nc.gpsimd.dma_start(staged[0:P:8, WB_COL:PLANE].bitcast(I32), wb_scales[0].bitcast(I32))
+        rw_t = tile("rw_t", [Q, 4], F32)
+        qw_t = tile("qw_t", [Q, 1], F32)
+        nc.gpsimd.dma_start(rw_t[:], rw.rearrange("o (q i) -> (o q) i", i=4))
+        nc.gpsimd.dma_start(qw_t[:], qw.rearrange("o q -> q o"))
+
+        scaled = [tile(f"scaled{e}", [P, 2, PAD + J], F32) for e in range(2)]
+        for e in range(2):
+            nc.scalar.activation(scaled[e][:, :, PAD - 1 : PAD], zero[:], ACT.Copy)
+        nc.vector.memset(plane[:].bitcast(I32), 0)
+
+        x_scale_g = tile("x_scale_g", [P, J], U8)
+        nc.vector.tensor_copy(x_scale_g[:], x_scale_win[:].indirect(offsets[:]))
+        for s in range(2):
+            nc.vector.tensor_copy(
+                staged[:, s * R : (s + 1) * R].rearrange("p (t b i) -> p b t i", t=4, i=16),
+                w_scale_raw[s][:].rearrange("p (b i t) -> p b t i", t=4, i=16),
+            )
+        nc.vector.tensor_copy(staged[:, X_COL:WB_COL].bitcast(I32), x_scale_g[:].bitcast(I32))
+        for x in range(4):
+            nc.sync.dma_start(plane[32 * x : 32 * x + 4, :].bitcast(I32), staged[32 * x : 32 * x + 32 : 8, :].bitcast(I32))
+
+        for t in range(4):
+            nc.scalar.activation(scaled[t // 2][:, t % 2, PAD:], so_t[t // 2][:, t % 2, :], ACT.Copy, scale=fl_t[:, t : t + 1])
+        w_dealt = [tile(f"w_dealt{s}", [P, 2 * R], U8) for s in range(2)]
+        for s in (1, 0):
+            nc.scalar.copy(
+                w_dealt[s][:].bitcast(U16).rearrange("p (t b i) -> p b t i", t=4, i=8),
+                w_raw[s][:].bitcast(U16).rearrange("p (b i t) -> p b t i", t=4, i=8),
+            )
+
+        u2 = [tile(f"u2_{h}", [P, HALF, 4], BF16) for h in range(2)]
+
+        def step(e, h):
+            lo = PAD + HALF * h
+            nc.vector.scalar_tensor_tensor(
+                u2[h][:, :, 2 * e : 2 * e + 2],
+                scaled[e][:, :, lo - 1 : lo - 1 + HALF].rearrange("p t j -> p j t"),
+                -0.8,
+                scaled[e][:, :, lo : lo + HALF].rearrange("p t j -> p j t"),
+                ALU.mult,
+                ALU.add,
+            )
+
+        u_codes = [tile(f"u_codes{h}", [P, HALF], U32) for h in range(2)]
+        u_scales = [tile(f"u_scales{h}", [P, HALF], U8) for h in range(2)]
+
+        def quantize_u(h):
+            nc.vector.quantize_mx(u_codes[h][:].bitcast(E4M3), u_scales[h][:], u2[h][:].rearrange("p j t -> p (j t)"))
+
+        x_words = tile("x_words", [P, J], U32)
+        step(0, 0)
+        step(1, 0)
+        step(0, 1)
+        quantize_u(0)
+        nc.vector.tensor_copy(x_words[:], x_word_win[:].bitcast(U32).indirect(offsets[:]))
+        step(1, 1)
+        quantize_u(1)
+
+        acc = [ps.tile([P, 4, HALF], F32, name=f"acc{h}") for h in range(2)]
+
+        def first_layer(h, s, codes, scales, start, stop):
+            for t in range(4):
+                nc.tensor.matmul_mx(
+                    acc[h][:, t, :],
+                    lhsT=w_dealt[s][:, 2 * P * t : 2 * P * (t + 1)].bitcast(E2M1),
+                    lhsT_scale=plane[:, s * R + P * t : s * R + P * (t + 1)],
+                    rhs=codes,
+                    rhs_scale=scales,
+                    start=start and t == 0,
+                    stop=stop and t == 3,
+                )
+
+        def x_part(h, start):
+            cols = slice(HALF * h, HALF * (h + 1))
+            first_layer(h, 0, x_words[:, cols].bitcast(E5M2), plane[:, X_COL + HALF * h : X_COL + HALF * (h + 1)], start, not start)
+
+        def u_part(h, start):
+            first_layer(h, 1, u_codes[h][:].bitcast(E4M3), u_scales[h][:], start, not start)
+
+        u_part(0, True)
+        x_part(0, False)
+        x_part(1, True)
+        u_part(1, False)
+
+        ident = tile("ident", [P, P], F32)
+        make_identity(nc, ident[:])
+        cw = tile("cw", [P, 4], F32)
+        nc.gpsimd.memset(cw[Q:P, :], 0.0)
+        nc.gpsimd.tensor_scalar(cw[0:Q, :], rw_t[:], qw_t[:, 0:1], None, ALU.mult)
+        cw_ps = ps.tile([P, 4, P], F32, name="cw_ps")
+        for i in range(4):
+            nc.tensor.transpose(cw_ps[:, i, :], cw[:, i : i + 1].to_broadcast([P, P]), ident[:])
+        cw_all = tile("cw_all", [P, Q, 4], F32)
+        nc.vector.tensor_copy(cw_all[:], cw_ps[:, :, 0:Q].rearrange("p i q -> p q i"))
+
+        out_rows = out.rearrange("(u p) q -> p u q", p=P)
+        hid = [tile(f"hid{h}", [P, HALF, 4], BF16) for h in range(2)]
+        h_codes = [tile(f"h_codes{h}", [P, HALF], U32) for h in range(2)]
+        h_scales = [tile(f"h_scales{h}", [P, HALF], U8) for h in range(2)]
+        prod = [ps.tile([P, 2, HALF], F32, name=f"prod{h}") for h in range(2)]
+        weighted = [tile(f"weighted{h}", [P, 2, HALF], F32) for h in range(2)]
+        sums = [tile(f"sums{h}", [P, 2, HALF // 4], F32) for h in range(2)]
+        for h in range(2):
+            nc.scalar.activation(hid[h][:], acc[h][:].rearrange("p t j -> p j t"), ACT.Relu)
+            nc.vector.quantize_mx(h_codes[h][:].bitcast(E5M2), h_scales[h][:], hid[h][:].rearrange("p j t -> p (j t)"))
+            for u in range(2):
+                nc.tensor.matmul_mx(
+                    prod[h][:, u, :],
+                    lhsT=wb_t[:, P * u : P * (u + 1)].bitcast(E4M3),
+                    lhsT_scale=plane[:, WB_COL + P * u : WB_COL + P * (u + 1)],
+                    rhs=h_codes[h][:].bitcast(E5M2),
+                    rhs_scale=h_scales[h][:],
+                    start=True,
+                    stop=True,
+                )
+        for h in range(2):
+            weights = cw_all[:].rearrange("p q i -> p (q i)")[:, HALF * h : HALF * (h + 1)]
+            nc.vector.tensor_tensor(weighted[h][:], prod[h][:], weights.unsqueeze(1).to_broadcast([P, 2, HALF]), ALU.mult)
+        for h in range(2):
+            nc.vector.tensor_reduce(
+                sums[h][:], weighted[h][:].rearrange("p u (q i) -> p u q i", i=4), mybir.AxisListType.X, ALU.add
+            )
+            nc.sync.dma_start(out_rows[:, :, 32 * h : 32 * (h + 1)], sums[h][:])

@@ -21,7 +21,7 @@ ACT = mybir.ActivationFunctionType
 P = 128
 HALF = 128
 PAD = 4
-W_COL, W2_COL, X_COL, WB_COL, PLANE = 0, 512, 1024, 1280, 1536
+X_COL, WB_COL, SLOT = 512, 768, 896
 
 
 def tile_list_sum_headpicks_stepped_plain_groupsums_kernel(
@@ -32,41 +32,43 @@ def tile_list_sum_headpicks_stepped_plain_groupsums_kernel(
         sb = ctx.enter_context(tc.tile_pool(name="sb", bufs=1))
         ps = ctx.enter_context(tc.psum_pool(name="ps", bufs=1))
 
-        def tile(name, shape, dtype):
-            return sb.tile(shape, dtype, name=name, align_bytes=64)
+        def tile(name, shape, dtype, tag=None):
+            return sb.tile(shape, dtype, name=name, tag=tag or name, align_bytes=64)
 
         offsets = sb.tile([P, J // 16], U16, name="offsets")
         nc.sync.dma_start(offsets[:], offs)
 
         x_scale_win = tile("x_scale_win", [P, T], U8)
-        w_scale_raw = [tile(f"w_scale_raw{s}", [P, R], U8) for s in range(2)]
-        staged = tile("staged", [P, PLANE], U8)
-        plane = tile("plane", [P, PLANE], U8)
+        w_scale_raw = tile("w_scale_raw", [P, R], U8)
+        staged = tile("staged", [P, SLOT], U8)
+        plane = tile("plane", [P, 2 * SLOT], U8)
+        nc.vector.memset(w_scale_raw[:].bitcast(I32), 0)
         zero = tile("zero", [P, 2, 1], F32)
         nc.vector.memset(zero[:], 0.0)
         nc.sync.dma_start(x_scale_win[:].bitcast(I32), xt_scales[0].bitcast(I32).unsqueeze(1).to_broadcast([16, 8, T // 4]))
+        for s, scales in enumerate((w_scales, w2_scales)):
+            nc.sync.dma_start(w_scale_raw[4 * s : P : 8, :].bitcast(I32), scales[0].bitcast(I32))
+
         fl_t = tile("fl_t", [P, 4], F32)
         nc.sync.dma_start(fl_t[:], fl.rearrange("(p t) o -> p (t o)", t=4))
-        for s, scales in enumerate((w_scales, w2_scales)):
-            nc.scalar.dma_start(w_scale_raw[s][:].bitcast(I32), scales[0].bitcast(I32).unsqueeze(1).to_broadcast([16, 8, R // 4]))
-
         so_rows = so.rearrange("(p t) j -> p t j", t=4)
         so_t = [tile(f"so{e}", [P, 2, J], F32) for e in range(2)]
         for e in range(2):
             nc.sync.dma_start(so_t[e][:], so_rows[:, 2 * e : 2 * e + 2, :])
         w_raw = [tile(f"w_raw{s}", [P, 2 * R], U8) for s in range(2)]
-        for s, words in ((1, w2_words), (0, w_words)):
-            nc.sync.dma_start(w_raw[s][:].bitcast(I32), words[0].bitcast(I32))
+        nc.sync.dma_start(w_raw[1][:].bitcast(I32), w2_words[0].bitcast(I32))
+        nc.sync.dma_start(staged[0:P:4, WB_COL:SLOT].bitcast(I32), wb_scales[0].rearrange("r (u n) -> (r u) n", u=2).bitcast(I32))
+        rw_t = tile("rw_t", [P, 2], F32)
+        qw_t = tile("qw_t", [P, 1], F32)
+        with nc.allow_non_contiguous_dma(reason="each set's weight goes to two partitions"):
+            nc.sync.dma_start(qw_t[:], qw[0].unsqueeze(1).to_broadcast([Q, 2]))
+        nc.sync.dma_start(w_raw[0][:].bitcast(I32), w_words[0].bitcast(I32))
         x_word_win = tile("x_word_win", [P, T], I32)
         nc.sync.dma_start(x_word_win[:], xt_words[0].rearrange("p n t -> p (n t)").bitcast(I32))
         wb_t = tile("wb_t", [P, N], I32)
-        nc.sync.dma_start(wb_t[:], wb_words[0].rearrange("p n t -> p (n t)").bitcast(I32))
 
-        nc.gpsimd.dma_start(staged[0:P:8, WB_COL:PLANE].bitcast(I32), wb_scales[0].bitcast(I32))
-        rw_t = tile("rw_t", [Q, 4], F32)
-        qw_t = tile("qw_t", [Q, 1], F32)
-        nc.gpsimd.dma_start(rw_t[:], rw.rearrange("o (q i) -> (o q) i", i=4))
-        nc.gpsimd.dma_start(qw_t[:], qw.rearrange("o q -> q o"))
+        nc.gpsimd.dma_start(rw_t[:], rw.rearrange("o (p e) -> (o p) e", e=2))
+        nc.gpsimd.dma_start(wb_t[:], wb_words[0].rearrange("p n t -> p (n t)").bitcast(I32))
 
         scaled = [tile(f"scaled{e}", [P, 2, PAD + J], F32) for e in range(2)]
         for e in range(2):
@@ -75,14 +77,13 @@ def tile_list_sum_headpicks_stepped_plain_groupsums_kernel(
 
         x_scale_g = tile("x_scale_g", [P, J], U8)
         nc.vector.tensor_copy(x_scale_g[:], x_scale_win[:].indirect(offsets[:]))
-        for s in range(2):
-            nc.vector.tensor_copy(
-                staged[:, s * R : (s + 1) * R].rearrange("p (t b i) -> p b t i", t=4, i=16),
-                w_scale_raw[s][:].rearrange("p (b i t) -> p b t i", t=4, i=16),
-            )
+        nc.vector.tensor_copy(
+            staged[:, 0:R].rearrange("p (t b i) -> p b t i", t=4, i=16),
+            w_scale_raw[:].rearrange("p (b i t) -> p b t i", t=4, i=16),
+        )
         nc.vector.tensor_copy(staged[:, X_COL:WB_COL].bitcast(I32), x_scale_g[:].bitcast(I32))
         for x in range(4):
-            nc.sync.dma_start(plane[32 * x : 32 * x + 4, :].bitcast(I32), staged[32 * x : 32 * x + 32 : 8, :].bitcast(I32))
+            nc.sync.dma_start(plane[32 * x : 32 * x + 4, :].bitcast(I32).rearrange("r (s c) -> r s c", s=2), staged[32 * x : 32 * x + 32 : 4, :].bitcast(I32))
 
         for t in range(4):
             nc.scalar.activation(scaled[t // 2][:, t % 2, PAD:], so_t[t // 2][:, t % 2, :], ACT.Copy, scale=fl_t[:, t : t + 1])
@@ -93,12 +94,13 @@ def tile_list_sum_headpicks_stepped_plain_groupsums_kernel(
                 w_raw[s][:].bitcast(U16).rearrange("p (b i t) -> p b t i", t=4, i=8),
             )
 
-        u2 = [tile(f"u2_{h}", [P, HALF, 4], BF16) for h in range(2)]
+        u2_all = tile("u2_all", [P, 4 * J], BF16)
+        u2 = [u2_all[:, 4 * HALF * h : 4 * HALF * (h + 1)] for h in range(2)]
 
         def step(e, h):
             lo = PAD + HALF * h
             nc.vector.scalar_tensor_tensor(
-                u2[h][:, :, 2 * e : 2 * e + 2],
+                u2[h].rearrange("p (j t) -> p j t", t=4)[:, :, 2 * e : 2 * e + 2],
                 scaled[e][:, :, lo - 1 : lo - 1 + HALF].rearrange("p t j -> p j t"),
                 -0.8,
                 scaled[e][:, :, lo : lo + HALF].rearrange("p t j -> p j t"),
@@ -110,15 +112,15 @@ def tile_list_sum_headpicks_stepped_plain_groupsums_kernel(
         u_scales = [tile(f"u_scales{h}", [P, HALF], U8) for h in range(2)]
 
         def quantize_u(h):
-            nc.vector.quantize_mx(u_codes[h][:].bitcast(E4M3), u_scales[h][:], u2[h][:].rearrange("p j t -> p (j t)"))
+            nc.vector.quantize_mx(u_codes[h][:].bitcast(E4M3), u_scales[h][:], u2[h])
 
         x_words = tile("x_words", [P, J], U32)
         step(0, 0)
-        step(1, 0)
         step(0, 1)
+        step(1, 0)
+        step(1, 1)
         quantize_u(0)
         nc.vector.tensor_copy(x_words[:], x_word_win[:].bitcast(U32).indirect(offsets[:]))
-        step(1, 1)
         quantize_u(1)
 
         acc = [ps.tile([P, 4, HALF], F32, name=f"acc{h}") for h in range(2)]
@@ -128,7 +130,7 @@ def tile_list_sum_headpicks_stepped_plain_groupsums_kernel(
                 nc.tensor.matmul_mx(
                     acc[h][:, t, :],
                     lhsT=w_dealt[s][:, 2 * P * t : 2 * P * (t + 1)].bitcast(E2M1),
-                    lhsT_scale=plane[:, s * R + P * t : s * R + P * (t + 1)],
+                    lhsT_scale=plane[:, s * SLOT + P * t : s * SLOT + P * (t + 1)],
                     rhs=codes,
                     rhs_scale=scales,
                     start=start and t == 0,
@@ -149,21 +151,20 @@ def tile_list_sum_headpicks_stepped_plain_groupsums_kernel(
 
         ident = tile("ident", [P, P], F32)
         make_identity(nc, ident[:])
-        cw = tile("cw", [P, 4], F32)
-        nc.gpsimd.memset(cw[Q:P, :], 0.0)
-        nc.gpsimd.tensor_scalar(cw[0:Q, :], rw_t[:], qw_t[:, 0:1], None, ALU.mult)
-        cw_ps = ps.tile([P, 4, P], F32, name="cw_ps")
-        for i in range(4):
+        cw = tile("cw", [P, 2], F32)
+        nc.gpsimd.tensor_scalar(cw[:], rw_t[:], qw_t[:, 0:1], None, ALU.mult)
+        cw_ps = ps.tile([P, 2, P], F32, name="cw_ps")
+        for i in range(2):
             nc.tensor.transpose(cw_ps[:, i, :], cw[:, i : i + 1].to_broadcast([P, P]), ident[:])
-        cw_all = tile("cw_all", [P, Q, 4], F32)
-        nc.vector.tensor_copy(cw_all[:], cw_ps[:, :, 0:Q].rearrange("p i q -> p q i"))
+        cw_all = tile("cw_all", [P, P, 2], F32)
+        nc.scalar.copy(cw_all[:], cw_ps[:].rearrange("p i q -> p q i"))
 
         out_rows = out.rearrange("(u p) q -> p u q", p=P)
         hid = [tile(f"hid{h}", [P, HALF, 4], BF16) for h in range(2)]
         h_codes = [tile(f"h_codes{h}", [P, HALF], U32) for h in range(2)]
         h_scales = [tile(f"h_scales{h}", [P, HALF], U8) for h in range(2)]
         prod = [ps.tile([P, 2, HALF], F32, name=f"prod{h}") for h in range(2)]
-        weighted = [tile(f"weighted{h}", [P, 2, HALF], F32) for h in range(2)]
+        weighted = [tile(f"weighted{h}", [P, 2, HALF], F32, tag=f"hid{1 - h}") for h in range(2)]
         sums = [tile(f"sums{h}", [P, 2, HALF // 4], F32) for h in range(2)]
         for h in range(2):
             nc.scalar.activation(hid[h][:], acc[h][:].rearrange("p t j -> p j t"), ACT.Relu)
@@ -172,7 +173,7 @@ def tile_list_sum_headpicks_stepped_plain_groupsums_kernel(
                 nc.tensor.matmul_mx(
                     prod[h][:, u, :],
                     lhsT=wb_t[:, P * u : P * (u + 1)].bitcast(E4M3),
-                    lhsT_scale=plane[:, WB_COL + P * u : WB_COL + P * (u + 1)],
+                    lhsT_scale=plane[:, SLOT * u + WB_COL : SLOT * (u + 1)],
                     rhs=h_codes[h][:].bitcast(E5M2),
                     rhs_scale=h_scales[h][:],
                     start=True,

from contextlib import ExitStack

import concourse.mybir as mybir
from concourse.masks import make_identity

K, T, J, R, F, N, Q = 512, 512, 256, 512, 512, 256, 64
FLOPS = 2 * (K * R * J + F * R * J + R * N * J)

F32 = mybir.dt.float32
BF16 = mybir.dt.bfloat16
I32 = mybir.dt.int32
U32 = mybir.dt.uint32
U16 = mybir.dt.uint16
U8 = mybir.dt.uint8
E4M3 = mybir.dt.float8_e4m3fn_x4
E5M2 = mybir.dt.float8_e5m2_x4
E2M1 = mybir.dt.float4_e2m1fn_x4
ALU = mybir.AluOpType
ACT = mybir.ActivationFunctionType

P = 128
HALF = 128
PAD = 4
X_COL, WB_COL, SLOT = 512, 768, 896


def tile_list_sum_headpicks_stepped_plain_groupsums_kernel(
    tc, xt_words, xt_scales, w_words, w_scales, so, fl, w2_words, w2_scales, wb_words, wb_scales, rw, qw, offs, out
):
    nc = tc.nc
    with ExitStack() as ctx:
        sb = ctx.enter_context(tc.tile_pool(name="sb", bufs=1))
        ps = ctx.enter_context(tc.psum_pool(name="ps", bufs=1))

        def tile(name, shape, dtype, tag=None):
            return sb.tile(shape, dtype, name=name, tag=tag or name, align_bytes=64)

        offsets = sb.tile([P, J // 16], U16, name="offsets")
        nc.sync.dma_start(offsets[:], offs)

        x_scale_win = tile("x_scale_win", [P, T], U8)
        w_scale_raw = tile("w_scale_raw", [P, R], U8)
        staged = tile("staged", [P, SLOT], U8)
        plane = tile("plane", [P, 2 * SLOT], U8)
        nc.vector.memset(w_scale_raw[:].bitcast(I32), 0)
        zero = tile("zero", [P, 2, 1], F32)
        nc.vector.memset(zero[:], 0.0)
        nc.sync.dma_start(x_scale_win[:].bitcast(I32), xt_scales[0].bitcast(I32).unsqueeze(1).to_broadcast([16, 8, T // 4]))
        for s, scales in enumerate((w_scales, w2_scales)):
            nc.sync.dma_start(w_scale_raw[4 * s : P : 8, :].bitcast(I32), scales[0].bitcast(I32))

        fl_t = tile("fl_t", [P, 4], F32)
        nc.sync.dma_start(fl_t[:], fl.rearrange("(p t) o -> p (t o)", t=4))
        so_rows = so.rearrange("(p t) j -> p t j", t=4)
        so_t = [tile(f"so{e}", [P, 2, J], F32) for e in range(2)]
        for e in range(2):
            nc.sync.dma_start(so_t[e][:], so_rows[:, 2 * e : 2 * e + 2, :])
        w_raw = [tile(f"w_raw{s}", [P, 2 * R], U8) for s in range(2)]
        nc.sync.dma_start(w_raw[1][:].bitcast(I32), w2_words[0].bitcast(I32))
        nc.sync.dma_start(staged[0:P:4, WB_COL:SLOT].bitcast(I32), wb_scales[0].rearrange("r (u n) -> (r u) n", u=2).bitcast(I32))
        rw_t = tile("rw_t", [P, 2], F32)
        qw_t = tile("qw_t", [P, 1], F32)
        with nc.allow_non_contiguous_dma(reason="each set's weight goes to two partitions"):
            nc.sync.dma_start(qw_t[:], qw[0].unsqueeze(1).to_broadcast([Q, 2]))
        nc.sync.dma_start(w_raw[0][:].bitcast(I32), w_words[0].bitcast(I32))
        x_word_win = tile("x_word_win", [P, T], I32)
        nc.sync.dma_start(x_word_win[:], xt_words[0].rearrange("p n t -> p (n t)").bitcast(I32))
        wb_t = tile("wb_t", [P, N], I32)

        nc.gpsimd.dma_start(rw_t[:], rw.rearrange("o (p e) -> (o p) e", e=2))
        nc.gpsimd.dma_start(wb_t[:], wb_words[0].rearrange("p n t -> p (n t)").bitcast(I32))

        scaled = [tile(f"scaled{e}", [P, 2, PAD + J], F32) for e in range(2)]
        for e in range(2):
            nc.scalar.activation(scaled[e][:, :, PAD - 1 : PAD], zero[:], ACT.Copy)
        nc.vector.memset(plane[:].bitcast(I32), 0)

        x_scale_g = tile("x_scale_g", [P, J], U8)
        nc.vector.tensor_copy(x_scale_g[:], x_scale_win[:].indirect(offsets[:]))
        nc.vector.tensor_copy(
            staged[:, 0:R].rearrange("p (t b i) -> p b t i", t=4, i=16),
            w_scale_raw[:].rearrange("p (b i t) -> p b t i", t=4, i=16),
        )
        nc.vector.tensor_copy(staged[:, X_COL:WB_COL].bitcast(I32), x_scale_g[:].bitcast(I32))
        for x in range(4):
            nc.sync.dma_start(plane[32 * x : 32 * x + 4, :].bitcast(I32).rearrange("r (s c) -> r s c", s=2), staged[32 * x : 32 * x + 32 : 4, :].bitcast(I32))

        for t in range(4):
            nc.scalar.activation(scaled[t // 2][:, t % 2, PAD:], so_t[t // 2][:, t % 2, :], ACT.Copy, scale=fl_t[:, t : t + 1])
        w_dealt = [tile(f"w_dealt{s}", [P, 2 * R], U8) for s in range(2)]
        for s in (1, 0):
            nc.scalar.copy(
                w_dealt[s][:].bitcast(U16).rearrange("p (t b i) -> p b t i", t=4, i=8),
                w_raw[s][:].bitcast(U16).rearrange("p (b i t) -> p b t i", t=4, i=8),
            )

        u2_all = tile("u2_all", [P, 4 * J], BF16)
        u2 = [u2_all[:, 4 * HALF * h : 4 * HALF * (h + 1)] for h in range(2)]

        def step(e, h):
            lo = PAD + HALF * h
            nc.vector.scalar_tensor_tensor(
                u2[h].rearrange("p (j t) -> p j t", t=4)[:, :, 2 * e : 2 * e + 2],
                scaled[e][:, :, lo - 1 : lo - 1 + HALF].rearrange("p t j -> p j t"),
                -0.8,
                scaled[e][:, :, lo : lo + HALF].rearrange("p t j -> p j t"),
                ALU.mult,
                ALU.add,
            )

        u_codes = [tile(f"u_codes{h}", [P, HALF], U32) for h in range(2)]
        u_scales = [tile(f"u_scales{h}", [P, HALF], U8) for h in range(2)]

        def quantize_u(h):
            nc.vector.quantize_mx(u_codes[h][:].bitcast(E4M3), u_scales[h][:], u2[h])

        x_words = tile("x_words", [P, J], U32)
        step(0, 0)
        step(0, 1)
        step(1, 0)
        step(1, 1)
        quantize_u(0)
        nc.vector.tensor_copy(x_words[:], x_word_win[:].bitcast(U32).indirect(offsets[:]))
        quantize_u(1)

        acc = [ps.tile([P, 4, HALF], F32, name=f"acc{h}") for h in range(2)]

        def first_layer(h, s, codes, scales, start, stop):
            for t in range(4):
                nc.tensor.matmul_mx(
                    acc[h][:, t, :],
                    lhsT=w_dealt[s][:, 2 * P * t : 2 * P * (t + 1)].bitcast(E2M1),
                    lhsT_scale=plane[:, s * SLOT + P * t : s * SLOT + P * (t + 1)],
                    rhs=codes,
                    rhs_scale=scales,
                    start=start and t == 0,
                    stop=stop and t == 3,
                )

        def x_part(h, start):
            cols = slice(HALF * h, HALF * (h + 1))
            first_layer(h, 0, x_words[:, cols].bitcast(E5M2), plane[:, X_COL + HALF * h : X_COL + HALF * (h + 1)], start, not start)

        def u_part(h, start):
            first_layer(h, 1, u_codes[h][:].bitcast(E4M3), u_scales[h][:], start, not start)

        u_part(0, True)
        x_part(0, False)
        x_part(1, True)
        u_part(1, False)

        ident = tile("ident", [P, P], F32)
        make_identity(nc, ident[:])
        cw = tile("cw", [P, 2], F32)
        nc.gpsimd.tensor_scalar(cw[:], rw_t[:], qw_t[:, 0:1], None, ALU.mult)
        cw_ps = ps.tile([P, 2, P], F32, name="cw_ps")
        for i in range(2):
            nc.tensor.transpose(cw_ps[:, i, :], cw[:, i : i + 1].to_broadcast([P, P]), ident[:])
        cw_all = tile("cw_all", [P, P, 2], F32)
        nc.scalar.copy(cw_all[:], cw_ps[:].rearrange("p i q -> p q i"))

        out_rows = out.rearrange("(u p) q -> p u q", p=P)
        hid = [tile(f"hid{h}", [P, HALF, 4], BF16) for h in range(2)]
        h_codes = [tile(f"h_codes{h}", [P, HALF], U32) for h in range(2)]
        h_scales = [tile(f"h_scales{h}", [P, HALF], U8) for h in range(2)]
        prod = [ps.tile([P, 2, HALF], F32, name=f"prod{h}") for h in range(2)]
        weighted = [tile(f"weighted{h}", [P, 2, HALF], F32, tag=f"hid{1 - h}") for h in range(2)]
        sums = [tile(f"sums{h}", [P, 2, HALF // 4], F32) for h in range(2)]
        for h in range(2):
            nc.scalar.activation(hid[h][:], acc[h][:].rearrange("p t j -> p j t"), ACT.Relu)
            nc.vector.quantize_mx(h_codes[h][:].bitcast(E5M2), h_scales[h][:], hid[h][:].rearrange("p j t -> p (j t)"))
            for u in range(2):
                nc.tensor.matmul_mx(
                    prod[h][:, u, :],
                    lhsT=wb_t[:, P * u : P * (u + 1)].bitcast(E4M3),
                    lhsT_scale=plane[:, SLOT * u + WB_COL : SLOT * (u + 1)],
                    rhs=h_codes[h][:].bitcast(E5M2),
                    rhs_scale=h_scales[h][:],
                    start=True,
                    stop=True,
                )
        for h in range(2):
            weights = cw_all[:].rearrange("p q i -> p (q i)")[:, HALF * h : HALF * (h + 1)]
            nc.vector.tensor_tensor(weighted[h][:], prod[h][:], weights.unsqueeze(1).to_broadcast([P, 2, HALF]), ALU.mult)
        for h in range(2):
            nc.vector.tensor_reduce(
                sums[h][:], weighted[h][:].rearrange("p u (q i) -> p u q i", i=4), mybir.AxisListType.X, ALU.add
            )
            nc.sync.dma_start(out_rows[:, :, 32 * h : 32 * (h + 1)], sums[h][:])
